import numpy as np
import ml_dtypes

BF16 = ml_dtypes.bfloat16


def bf(x):
    return np.asarray(x, np.float32).astype(BF16)


def f32(x):
    return np.asarray(x, np.float32)


def f64(x):
    return np.asarray(x).astype(np.float64)


def striped(idx):
    return np.tile(idx.reshape(-1, 16).T, (8, 1))


S, K, N, V, D, H, O = 1024, 128, 256, 128, 2, 128, 256


def sigmoid(v):
    return 1.0 / (1.0 + np.exp(-v))


def setup_inputs():
    return {"table": bf(np.random.standard_normal((K, S))), "w": bf(np.random.standard_normal((D, K, H)) / np.sqrt(D * K)), "b": f32(0.5 * np.random.standard_normal((H, 1))), "w2": bf(np.random.standard_normal((H, O)) / np.sqrt(H)), "offs": striped(np.random.permutation(S)[:N])}


def reference(table, w, b, w2, offs):
    idx = offs[:16].T.reshape(-1)
    x = f64(table)[:, idx]
    t = sum(f64(w)[d].T @ x[:, d * V : (d + 1) * V] for d in range(D)) + f64(b)
    t = t * sigmoid(t)
    return f64(w2).T @ t

@@ -1,0 +1,48 @@
+import concourse.mybir as mybir
+
+BF16, F32, U16 = mybir.dt.bfloat16, mybir.dt.float32, mybir.dt.uint16
+SILU = mybir.ActivationFunctionType.Silu
+
+P = 128
+FLOPS = 2 * 2 * 128 * 128 * 128 + 2 * 128 * 256 * 128
+
+
+def tile_rows_edge2_silu_sub_kernel(tc, table, w, b, w2, offs, out):
+    nc = tc.nc
+    features, nodes = table.shape
+    ends, hidden = w.shape[0], w.shape[2]
+    outputs, edges = out.shape
+    blocks = outputs // P
+    columns = edges // 16
+
+    with (
+        tc.tile_pool(name="held", bufs=1) as held,
+        tc.psum_pool(name="psum", bufs=1) as psum,
+    ):
+        table_tile = held.tile([features, nodes], BF16, name="table_tile")
+        offsets = held.tile([P, ends * columns], U16, name="offsets")
+        w_tile = held.tile([features, ends, hidden], BF16, name="w_tile")
+        bias = held.tile([hidden, 1], F32, name="bias")
+        w2_tile = held.tile([hidden, outputs], BF16, name="w2_tile")
+
+        nc.sync.dma_start(table_tile[:], table)
+        nc.sync.dma_start(offsets[:], offs)
+        nc.scalar.dma_start(w_tile[:], w.rearrange("d k i -> k d i"))
+        nc.scalar.dma_start(bias[:], b)
+        nc.scalar.dma_start(w2_tile[:], w2)
+
+        layer1 = psum.tile([hidden, edges], F32, name="layer1")
+        for d in range(ends):
+            picked = table_tile[:].indirect(offsets[:, d * columns : (d + 1) * columns])
+            nc.tensor.matmul(layer1[:], w_tile[:, d, :], picked, start=(d == 0), stop=(d == ends - 1))
+
+        h = held.tile([hidden, edges], BF16, name="h")
+        nc.scalar.activation(h[:], layer1[:], SILU, bias=bias[:])
+
+        layer2 = psum.tile([P, blocks, edges], F32, name="layer2")
+        for a in range(blocks):
+            nc.tensor.matmul(layer2[:, a, :], w2_tile[:, a * P : (a + 1) * P], h[:], start=True, stop=True)
+
+        result = held.tile([P, blocks, edges], F32, name="result")
+        nc.vector.tensor_copy(result[:], layer2[:])
+        nc.sync.dma_start(out.rearrange("(a p) v -> p a v", p=P), result[:])

@@ -31,6 +31,11 @@ def tile_rows_edge2_silu_sub_kernel(tc, table, w, b, w2, offs, out):
         nc.scalar.dma_start(bias[:], b)
         nc.scalar.dma_start(w2_tile[:], w2)
 
+        warm_in = held.tile([P, 1], F32, name="warm_in")
+        warm_out = held.tile([P, 1], F32, name="warm_out")
+        nc.vector.memset(warm_in[:], 0.0)
+        nc.scalar.activation(warm_out[:], warm_in[:], SILU)
+
         layer1 = psum.tile([hidden, edges], F32, name="layer1")
         for d in range(ends):
             picked = table_tile[:].indirect(offsets[:, d * columns : (d + 1) * columns])
@@ -39,10 +44,11 @@ def tile_rows_edge2_silu_sub_kernel(tc, table, w, b, w2, offs, out):
         h = held.tile([hidden, edges], BF16, name="h")
         nc.scalar.activation(h[:], layer1[:], SILU, bias=bias[:])
 
-        layer2 = psum.tile([P, blocks, edges], F32, name="layer2")
+        copies = (nc.vector.tensor_copy, nc.scalar.copy)
+        queues = (nc.sync, nc.scalar)
         for a in range(blocks):
-            nc.tensor.matmul(layer2[:, a, :], w2_tile[:, a * P : (a + 1) * P], h[:], start=True, stop=True)
-
-        result = held.tile([P, blocks, edges], F32, name="result")
-        nc.vector.tensor_copy(result[:], layer2[:])
-        nc.sync.dma_start(out.rearrange("(a p) v -> p a v", p=P), result[:])
+            layer2 = psum.tile([P, edges], F32, name=f"layer2_{a}")
+            result = held.tile([P, edges], F32, name=f"result_{a}")
+            nc.tensor.matmul(layer2[:], w2_tile[:, a * P : (a + 1) * P], h[:], start=True, stop=True)
+            copies[a](result[:], layer2[:])
+            queues[a].dma_start(out[a * P : (a + 1) * P, :], result[:])

@@ -28,8 +28,8 @@ def tile_rows_edge2_silu_sub_kernel(tc, table, w, b, w2, offs, out):
         nc.sync.dma_start(table_tile[:], table)
         nc.sync.dma_start(offsets[:], offs)
         nc.scalar.dma_start(w_tile[:], w.rearrange("d k i -> k d i"))
-        nc.scalar.dma_start(bias[:], b)
-        nc.scalar.dma_start(w2_tile[:], w2)
+        nc.sync.dma_start(bias[:], b)
+        nc.sync.dma_start(w2_tile[:], w2)
 
         warm_in = held.tile([P, 1], F32, name="warm_in")
         warm_out = held.tile([P, 1], F32, name="warm_out")

@@ -27,7 +27,7 @@ def tile_rows_edge2_silu_sub_kernel(tc, table, w, b, w2, offs, out):
 
         nc.sync.dma_start(table_tile[:], table)
         nc.sync.dma_start(offsets[:], offs)
-        nc.scalar.dma_start(w_tile[:], w.rearrange("d k i -> k d i"))
+        nc.sync.dma_start(w_tile[:], w.rearrange("d k i -> k d i"))
         nc.sync.dma_start(bias[:], b)
         nc.sync.dma_start(w2_tile[:], w2)
 
@@ -45,10 +45,9 @@ def tile_rows_edge2_silu_sub_kernel(tc, table, w, b, w2, offs, out):
         nc.scalar.activation(h[:], layer1[:], SILU, bias=bias[:])
 
         copies = (nc.vector.tensor_copy, nc.scalar.copy)
-        queues = (nc.sync, nc.scalar)
         for a in range(blocks):
             layer2 = psum.tile([P, edges], F32, name=f"layer2_{a}")
             result = held.tile([P, edges], F32, name=f"result_{a}")
             nc.tensor.matmul(layer2[:], w2_tile[:, a * P : (a + 1) * P], h[:], start=True, stop=True)
             copies[a](result[:], layer2[:])
-            queues[a].dma_start(out[a * P : (a + 1) * P, :], result[:])
+            nc.sync.dma_start(out[a * P : (a + 1) * P, :], result[:])

@@ -4,6 +4,7 @@ BF16, F32, U16 = mybir.dt.bfloat16, mybir.dt.float32, mybir.dt.uint16
 SILU = mybir.ActivationFunctionType.Silu
 
 P = 128
+WARM_COLUMNS, WARM_MATMULS = 256, 6
 FLOPS = 2 * 2 * 128 * 128 * 128 + 2 * 128 * 256 * 128
 
 
@@ -31,10 +32,13 @@ def tile_rows_edge2_silu_sub_kernel(tc, table, w, b, w2, offs, out):
         nc.sync.dma_start(bias[:], b)
         nc.sync.dma_start(w2_tile[:], w2)
 
-        warm_in = held.tile([P, 1], F32, name="warm_in")
-        warm_out = held.tile([P, 1], F32, name="warm_out")
-        nc.vector.memset(warm_in[:], 0.0)
-        nc.scalar.activation(warm_out[:], warm_in[:], SILU)
+        zeros = held.tile([P, WARM_COLUMNS], BF16, name="zeros")
+        warm_silu = held.tile([P, 1], F32, name="warm_silu")
+        warm_bank = psum.tile([P, WARM_COLUMNS], F32, name="warm_bank")
+        nc.vector.memset(zeros[:], 0.0)
+        nc.scalar.activation(warm_silu[:], zeros[:, 0:1], SILU)
+        for step in range(WARM_MATMULS):
+            nc.tensor.matmul(warm_bank[:], zeros[:, 0:P], zeros[:], start=True, stop=True)
 
         layer1 = psum.tile([hidden, edges], F32, name="layer1")
         for d in range(ends):

import concourse.mybir as mybir

BF16, F32, U16 = mybir.dt.bfloat16, mybir.dt.float32, mybir.dt.uint16
SILU = mybir.ActivationFunctionType.Silu

P = 128
WARM_COLUMNS, WARM_MATMULS = 256, 6
FLOPS = 2 * 2 * 128 * 128 * 128 + 2 * 128 * 256 * 128


def tile_rows_edge2_silu_sub_kernel(tc, table, w, b, w2, offs, out):
    nc = tc.nc
    features, nodes = table.shape
    ends, hidden = w.shape[0], w.shape[2]
    outputs, edges = out.shape
    blocks = outputs // P
    columns = edges // 16

    with (
        tc.tile_pool(name="held", bufs=1) as held,
        tc.psum_pool(name="psum", bufs=1) as psum,
    ):
        table_tile = held.tile([features, nodes], BF16, name="table_tile")
        offsets = held.tile([P, ends * columns], U16, name="offsets")
        w_tile = held.tile([features, ends, hidden], BF16, name="w_tile")
        bias = held.tile([hidden, 1], F32, name="bias")
        w2_tile = held.tile([hidden, outputs], BF16, name="w2_tile")

        nc.sync.dma_start(table_tile[:], table)
        nc.sync.dma_start(offsets[:], offs)
        nc.sync.dma_start(w_tile[:], w.rearrange("d k i -> k d i"))
        nc.sync.dma_start(bias[:], b)
        nc.sync.dma_start(w2_tile[:], w2)

        zeros = held.tile([P, WARM_COLUMNS], BF16, name="zeros")
        warm_silu = held.tile([P, 1], F32, name="warm_silu")
        warm_bank = psum.tile([P, WARM_COLUMNS], F32, name="warm_bank")
        nc.vector.memset(zeros[:], 0.0)
        nc.scalar.activation(warm_silu[:], zeros[:, 0:1], SILU)
        for step in range(WARM_MATMULS):
            nc.tensor.matmul(warm_bank[:], zeros[:, 0:P], zeros[:], start=True, stop=True)

        layer1 = psum.tile([hidden, edges], F32, name="layer1")
        for d in range(ends):
            picked = table_tile[:].indirect(offsets[:, d * columns : (d + 1) * columns])
            nc.tensor.matmul(layer1[:], w_tile[:, d, :], picked, start=(d == 0), stop=(d == ends - 1))

        h = held.tile([hidden, edges], BF16, name="h")
        nc.scalar.activation(h[:], layer1[:], SILU, bias=bias[:])

        copies = (nc.vector.tensor_copy, nc.scalar.copy)
        for a in range(blocks):
            layer2 = psum.tile([P, edges], F32, name=f"layer2_{a}")
            result = held.tile([P, edges], F32, name=f"result_{a}")
            nc.tensor.matmul(layer2[:], w2_tile[:, a * P : (a + 1) * P], h[:], start=True, stop=True)
            copies[a](result[:], layer2[:])
            nc.sync.dma_start(out[a * P : (a + 1) * P, :], result[:])
